import numpy as np
import ml_dtypes

BF16 = ml_dtypes.bfloat16


def bf(x):
    return np.asarray(x, np.float32).astype(BF16)


def f32(x):
    return np.asarray(x, np.float32)


def f64(x):
    return np.asarray(x).astype(np.float64)


def striped(idx):
    return np.tile(idx.reshape(-1, 16).T, (8, 1))


def rows(idx, k):
    return np.tile(idx, (k, 1))


def look(tab, idx):
    return np.take_along_axis(f64(tab), rows(idx, len(tab)), axis=1)


K, S, D, V, N, M = 128, 256, 3, 128, 384, 128


def setup_inputs():
    return {"tab": bf(0.7 * np.random.standard_normal((D, K, S))), "base": bf(np.random.standard_normal((K, V))), "w": bf(np.random.standard_normal((K, M)) / np.sqrt(K)), "b": f32(0.5 * np.random.standard_normal((M, 1))), "offs": striped(np.random.randint(0, S, N))}


def reference(tab, base, w, b, offs):
    idx = offs[:16].T.reshape(-1)
    x = f64(base) + sum(look(tab[d], idx[d * V:(d + 1) * V]) for d in range(D))
    y = f64(w).T @ x
    return np.maximum(y + f64(b), 0.0)

@@ -1,0 +1,50 @@
+import concourse.mybir as mybir
+
+BF16, F32, U16 = mybir.dt.bfloat16, mybir.dt.float32, mybir.dt.uint16
+ADD = mybir.AluOpType.add
+RELU = mybir.ActivationFunctionType.Relu
+
+STAGES, ROWS, CODEWORDS = 3, 128, 256
+VECTORS = 128
+FEATURES = 128
+LANES = 16
+LIST_COLUMNS = VECTORS // LANES
+
+FLOPS = 2 * ROWS * FEATURES * VECTORS
+
+
+def tile_lookup_res_add_relu_kernel(tc, tab, base, w, b, offs, out):
+    nc = tc.nc
+    with tc.tile_pool(name="sbuf", bufs=1) as sbuf, tc.psum_pool(name="psum", bufs=1) as psum:
+        offsets = sbuf.tile([ROWS, STAGES * LIST_COLUMNS], U16, name="offsets")
+        base_in = sbuf.tile([ROWS, VECTORS], BF16, name="base_in")
+        weights = sbuf.tile([ROWS, FEATURES], BF16, name="weights")
+        bias = sbuf.tile([FEATURES, 1], F32, name="bias")
+        book_in = [sbuf.tile([ROWS, CODEWORDS], BF16, name=f"book_in{d}") for d in range(STAGES)]
+        book = [sbuf.tile([ROWS, CODEWORDS], F32, name=f"book{d}") for d in range(STAGES)]
+        total = [sbuf.tile([ROWS, VECTORS], F32, name=f"total{d}") for d in range(STAGES + 1)]
+        x = sbuf.tile([ROWS, VECTORS], BF16, name="x")
+        result = sbuf.tile([FEATURES, VECTORS], F32, name="result")
+
+        nc.sync.dma_start(book_in[0][:], tab[0])
+        nc.scalar.dma_start(base_in[:], base)
+        nc.sync.dma_start(offsets[:], offs)
+        nc.scalar.dma_start(book_in[1][:], tab[1])
+        nc.sync.dma_start(book_in[2][:], tab[2])
+        nc.scalar.dma_start(weights[:], w)
+        nc.scalar.dma_start(bias[:], b)
+
+        nc.vector.tensor_copy(book[0][:], book_in[0][:])
+        nc.scalar.copy(total[0][:], base_in[:])
+        for d in range(1, STAGES):
+            nc.scalar.copy(book[d][:], book_in[d][:])
+
+        for d in range(STAGES):
+            entries = offsets[:, d * LIST_COLUMNS : (d + 1) * LIST_COLUMNS]
+            nc.vector.tensor_tensor(total[d + 1][:], book[d][:].indirect(entries), total[d][:], ADD)
+        nc.vector.tensor_copy(x[:], total[STAGES][:])
+
+        product = psum.tile([FEATURES, VECTORS], F32, name="product")
+        nc.tensor.matmul(product[:], weights[:], x[:], start=True, stop=True)
+        nc.scalar.activation(result[:], product[:], RELU, bias=bias[:])
+        nc.sync.dma_start(out, result[:])

@@ -35,7 +35,7 @@ def tile_lookup_res_add_relu_kernel(tc, tab, base, w, b, offs, out):
         nc.scalar.dma_start(bias[:], b)
 
         nc.vector.tensor_copy(book[0][:], book_in[0][:])
-        nc.scalar.copy(total[0][:], base_in[:])
+        nc.vector.tensor_copy(total[0][:], base_in[:])
         for d in range(1, STAGES):
             nc.scalar.copy(book[d][:], book_in[d][:])
 

import concourse.mybir as mybir

BF16, F32, U16 = mybir.dt.bfloat16, mybir.dt.float32, mybir.dt.uint16
ADD = mybir.AluOpType.add
RELU = mybir.ActivationFunctionType.Relu

STAGES, ROWS, CODEWORDS = 3, 128, 256
VECTORS = 128
FEATURES = 128
LANES = 16
LIST_COLUMNS = VECTORS // LANES

FLOPS = 2 * ROWS * FEATURES * VECTORS


def tile_lookup_res_add_relu_kernel(tc, tab, base, w, b, offs, out):
    nc = tc.nc
    with tc.tile_pool(name="sbuf", bufs=1) as sbuf, tc.psum_pool(name="psum", bufs=1) as psum:
        offsets = sbuf.tile([ROWS, STAGES * LIST_COLUMNS], U16, name="offsets")
        base_in = sbuf.tile([ROWS, VECTORS], BF16, name="base_in")
        weights = sbuf.tile([ROWS, FEATURES], BF16, name="weights")
        bias = sbuf.tile([FEATURES, 1], F32, name="bias")
        book_in = [sbuf.tile([ROWS, CODEWORDS], BF16, name=f"book_in{d}") for d in range(STAGES)]
        book = [sbuf.tile([ROWS, CODEWORDS], F32, name=f"book{d}") for d in range(STAGES)]
        total = [sbuf.tile([ROWS, VECTORS], F32, name=f"total{d}") for d in range(STAGES + 1)]
        x = sbuf.tile([ROWS, VECTORS], BF16, name="x")
        result = sbuf.tile([FEATURES, VECTORS], F32, name="result")

        nc.sync.dma_start(book_in[0][:], tab[0])
        nc.scalar.dma_start(base_in[:], base)
        nc.sync.dma_start(offsets[:], offs)
        nc.scalar.dma_start(book_in[1][:], tab[1])
        nc.sync.dma_start(book_in[2][:], tab[2])
        nc.scalar.dma_start(weights[:], w)
        nc.scalar.dma_start(bias[:], b)

        nc.vector.tensor_copy(book[0][:], book_in[0][:])
        nc.vector.tensor_copy(total[0][:], base_in[:])
        for d in range(1, STAGES):
            nc.scalar.copy(book[d][:], book_in[d][:])

        for d in range(STAGES):
            entries = offsets[:, d * LIST_COLUMNS : (d + 1) * LIST_COLUMNS]
            nc.vector.tensor_tensor(total[d + 1][:], book[d][:].indirect(entries), total[d][:], ADD)
        nc.vector.tensor_copy(x[:], total[STAGES][:])

        product = psum.tile([FEATURES, VECTORS], F32, name="product")
        nc.tensor.matmul(product[:], weights[:], x[:], start=True, stop=True)
        nc.scalar.activation(result[:], product[:], RELU, bias=bias[:])
        nc.sync.dma_start(out, result[:])
